import numpy as np, ml_dtypes
CORES = [129,145,193,257,273,321,385,401,449]
N = 9
TK = 128
def silu(z): return z / (1.0 + np.exp(-z))
def setup_inputs(rng):
    return {"x": rng.standard_normal((N, 128, TK), dtype=np.float32).astype(ml_dtypes.bfloat16), "w1": (rng.standard_normal((N, 128, 128), dtype=np.float32) / 8).astype(ml_dtypes.bfloat16), "w3": (rng.standard_normal((N, 128, 128), dtype=np.float32) / 8).astype(ml_dtypes.bfloat16), "w2": (rng.standard_normal((N, 128, 128), dtype=np.float32) / 8).astype(ml_dtypes.bfloat16)}
def setup_inputs_big(rng):
    d = setup_inputs(rng)
    for k in ("x",): d[k] = (d[k].astype(np.float32) * 1024.0).astype(d[k].dtype)
    return d
def setup_inputs_small(rng):
    d = setup_inputs(rng)
    for k in ("x",): d[k] = (d[k].astype(np.float32) * (1 / 1024.0)).astype(d[k].dtype)
    return d
def setup_inputs_apart(rng):
    d = setup_inputs(rng)
    f = (10.0 ** rng.permutation(np.linspace(-1.5, 1.5, N))).astype(np.float32).reshape(N, 1, 1)
    for k in ("x",): d[k] = (d[k].astype(np.float32) * f).astype(d[k].dtype)
    return d
def reference(x, w1, w3, w2):
    X, W1, W3, W2 = x.astype(np.float64), w1.astype(np.float64), w3.astype(np.float64), w2.astype(np.float64)
    y = np.zeros((N, 128, TK))
    for r in range(N):
        for j in range(N):
            y[r] += W2[j].T @ (silu(W1[j].T @ X[r]) * (W3[j].T @ X[r]))
    return {"y": y.astype(ml_dtypes.bfloat16)}

@@ -1,0 +1,168 @@
+from concourse.bass import DstId, RemoteDMATransfer
+from concourse.mybir import AluOpType, ActivationFunctionType
+
+D = 128
+WW = 3 * D
+NSLOT = 5
+
+SCRATCH = {
+    "xb": ("sbuf", [D, 2 * D], "bfloat16"),
+    "wo": ("sbuf", [D, WW], "bfloat16"),
+    "wl": ("sbuf", [D, NSLOT * WW], "bfloat16"),
+    "sl": ("sbuf", [D, 4 * D], "float32"),
+    "hb": ("sbuf", [D, 4 * D], "bfloat16"),
+    "po": ("sbuf", [D, D], "bfloat16"),
+    "pl": ("sbuf", [D, D], "bfloat16"),
+    "yb": ("sbuf", [D, D], "bfloat16"),
+    "z1a": ("psum", [D, 512], "float32"), "z1b": ("psum", [D, 512], "float32"),
+    "z3a": ("psum", [D, 512], "float32"), "z3b": ("psum", [D, 512], "float32"),
+    "ya": ("psum", [D, 512], "float32"),
+}
+SEMAPHORES = ["lx", "lw", "xin", "pin", "snd", "p1", "p3", "ac", "vh", "py", "vp", "vy", "st"] + ["wr%d" % i for i in range(9)]
+
+
+def _plan(T, topo):
+    ranks = list(T.cores)
+    both = lambda a, b: topo.may_write(a, b) and topo.may_write(b, a)
+    hosts = sorted(set(topo.host(c) for c in ranks))
+    of = lambda h: sorted((c for c in ranks if topo.host(c) == h), key=topo.chip)
+    hub = [h for h in hosts if all(both(a, b) for a in of(h) for b in ranks if a != b)][0]
+    ends = [h for h in hosts if h != hub]
+    hb = [h for h in ends if topo.rack(h) == topo.rack(hub)][0]
+    ha = [h for h in ends if h != hb][0]
+    A, M, B = of(ha), of(hub), of(hb)
+    Z = []
+    for b in B:
+        for h in range(4):
+            z = b + (h - topo.host(b)) * topo.CORES_PER_HOST
+            if h not in hosts and both(b, z) and all(topo.may_write(a, z) and topo.same_plane(a, z) for a in A):
+                Z.append(z)
+    n = len(A)
+    role = {}
+    for name, grp in (("A", A), ("M", M), ("B", B), ("Z", Z)):
+        for i, c in enumerate(grp):
+            role[c] = (name, i)
+    send = {}
+    for i, a in enumerate(A):
+        send[a] = [Z[(i + k) % n] for k in range(n)] + [A[(i + k) % n] for k in range(1, n)]
+    ring = M + B
+    for i, c in enumerate(ring):
+        send[c] = [ring[(i + k) % len(ring)] for k in range(1, len(ring))]
+    guest_to, part_to = {}, {}
+    for i in range(n):
+        guest_to[A[i]], guest_to[M[i]], guest_to[B[i]] = M[i], A[i], Z[i]
+        part_to[A[i]], part_to[M[i]], part_to[Z[i]] = M[i], A[i], B[i]
+    return role, send, guest_to, part_to
+
+
+def _arrivals(send, d):
+    return sorted((s for s in send if d in send[s]), key=lambda s: (send[s].index(d), s))
+
+
+def _engines(mask):
+    return bin(mask).count("1")
+
+
+def rank_program(g, core, T, topo):
+    role, send, guest_to, part_to = _plan(T, topo)
+    if core not in role:
+        return
+    S = T.sem
+    kind = role[core][0]
+    is_rank = kind != "Z"
+    hosts_guest = kind in ("A", "M")
+    n = 2 * D if hosts_guest else D
+    sent = 0
+
+    if is_rank:
+        g.sync.dma_start(T.xb[:, 0:D], T.x[:]).then_inc(S.lx, 16)
+        g.scalar.dma_start(T.wo[:, 0:D], T.w1[:]).then_inc(S.lw, 16)
+        g.sync.dma_start(T.wo[:, D:2 * D], T.w3[:]).then_inc(S.lw, 16)
+        g.scalar.dma_start(T.wo[:, 2 * D:WW], T.w2[:]).then_inc(S.lw, 16)
+
+    if is_rank:
+        d = guest_to[core]
+        rid, pid = topo.addr(d, core)
+        m = topo.mask(core, d)
+        col = 0 if role[d][0] == "Z" else D
+        g.wait_ge(S.lx, 16)
+        g.remote_dma(T.xb[:, col:col + D], T.xb[:, 0:D], S.xin, S.snd, pid, rid, m)
+        sent += _engines(m)
+        m = topo.mask(core, send[core][0])
+        ids, dsts = [], []
+        for d in send[core]:
+            m &= topo.mask(core, d)
+            rid, pid = topo.addr(d, core)
+            slot = _arrivals(send, d).index(core)
+            ids.append(DstId(rid=rid, pnc=pid))
+            dsts.append(T.wl[:, slot * WW:(slot + 1) * WW])
+        g.wait_ge(S.lw, 48)
+        g.remote_dma_fused([RemoteDMATransfer(dst_ids=ids, dma_engine_mask=m, remote_sem=S["wr%d" % T.rank_of(core)],
+                                              srcs=[T.wo[:]], dsts=dsts, alu_op=0)], local_sem=S.snd)
+        sent += _engines(m)
+
+    batches = []
+    first = []
+    if is_rank:
+        first += [(S.lx, 16), (S.lw, 48)]
+    if hosts_guest or not is_rank:
+        src = [s for s in guest_to if guest_to[s] == core][0]
+        first.append((S.xin, _engines(topo.mask(src, core))))
+    if is_rank:
+        batches.append((first, T.wo, 0))
+        first = []
+    for slot, s in enumerate(_arrivals(send, core)):
+        m = topo.mask(s, send[s][0])
+        for d in send[s]:
+            m &= topo.mask(s, d)
+        batches.append((first + [(S["wr%d" % T.rank_of(s)], _engines(m))], T.wl, slot * WW))
+        first = []
+    K = len(batches)
+    X = T.xb[:, 0:n]
+    z1, z3 = [T.z1a, T.z1b], [T.z3a, T.z3b]
+
+    def down(k):
+        o = (k % 2) * 2 * D
+        buf, c0 = batches[k][1], batches[k][2]
+        g.tensor.wait_ge(S.vh, k + 1)
+        g.tensor.matmul(T.ya[:, 0:n], buf[:, c0 + 2 * D:c0 + WW], T.hb[:, o:o + n], k == 0, k == K - 1).then_inc(S.py, 1)
+
+    for k in range(K):
+        waits, buf, c0 = batches[k]
+        o = (k % 2) * 2 * D
+        for sem, val in waits:
+            g.tensor.wait_ge(sem, val)
+        g.tensor.matmul(z1[k % 2][:, 0:n], buf[:, c0:c0 + D], X, True, True).then_inc(S.p1, 1)
+        g.tensor.matmul(z3[k % 2][:, 0:n], buf[:, c0 + D:c0 + 2 * D], X, True, True).then_inc(S.p3, 1)
+        if k >= 1:
+            down(k - 1)
+        g.scalar.wait_ge(S.p1, k + 1)
+        if k >= 2:
+            g.scalar.wait_ge(S.vh, k - 1)
+        g.scalar.activation(T.sl[:, o:o + n], z1[k % 2][:, 0:n], ActivationFunctionType.Silu).then_inc(S.ac, 1)
+        g.vector.wait_ge(S.ac, k + 1)
+        g.vector.wait_ge(S.p3, k + 1)
+        if k >= 2:
+            g.vector.wait_ge(S.py, k - 1)
+        g.vector.tensor_tensor(T.hb[:, o:o + n], T.sl[:, o:o + n], z3[k % 2][:, 0:n], AluOpType.mult).then_inc(S.vh, 1)
+    down(K - 1)
+
+    g.vector.wait_ge(S.py, K)
+    if core in part_to:
+        c0 = D if hosts_guest else 0
+        g.vector.tensor_copy(T.po[:], T.ya[:, c0:c0 + D]).then_inc(S.vp, 1)
+        d = part_to[core]
+        rid, pid = topo.addr(d, core)
+        m = topo.mask(core, d)
+        g.wait_ge(S.vp, 1)
+        g.remote_dma(T.pl[:], T.po[:], S.pin, S.snd, pid, rid, m)
+        sent += _engines(m)
+
+    if is_rank:
+        src = [s for s in part_to if part_to[s] == core][0]
+        g.vector.wait_ge(S.pin, _engines(topo.mask(src, core)))
+        g.vector.tensor_tensor(T.yb[:], T.ya[:, 0:D], T.pl[:], AluOpType.add).then_inc(S.vy, 1)
+        g.sync.wait_ge(S.vy, 1)
+        g.sync.dma_start(T.y[:], T.yb[:]).then_inc(S.st, 16)
+        g.sync.wait_ge(S.st, 16)
+    g.wait_ge(S.snd, sent)

@@ -4,21 +4,25 @@ from concourse.mybir import AluOpType, ActivationFunctionType
 D = 128
 WW = 3 * D
 NSLOT = 5
+NDIRECT = 3
+LAG = 2
+NB = 3
 
 SCRATCH = {
     "xb": ("sbuf", [D, 2 * D], "bfloat16"),
     "wo": ("sbuf", [D, WW], "bfloat16"),
     "wl": ("sbuf", [D, NSLOT * WW], "bfloat16"),
-    "sl": ("sbuf", [D, 4 * D], "float32"),
-    "hb": ("sbuf", [D, 4 * D], "bfloat16"),
+    "sl": ("sbuf", [D, NB * D], "float32"),
+    "hb": ("sbuf", [D, NB * D], "bfloat16"),
     "po": ("sbuf", [D, D], "bfloat16"),
     "pl": ("sbuf", [D, D], "bfloat16"),
     "yb": ("sbuf", [D, D], "bfloat16"),
-    "z1a": ("psum", [D, 512], "float32"), "z1b": ("psum", [D, 512], "float32"),
-    "z3a": ("psum", [D, 512], "float32"), "z3b": ("psum", [D, 512], "float32"),
+    "z1a": ("psum", [D, 512], "float32"), "z1b": ("psum", [D, 512], "float32"), "z1c": ("psum", [D, 512], "float32"),
+    "z3a": ("psum", [D, 512], "float32"), "z3b": ("psum", [D, 512], "float32"), "z3c": ("psum", [D, 512], "float32"),
     "ya": ("psum", [D, 512], "float32"),
+    "yg": ("psum", [D, 512], "float32"),
 }
-SEMAPHORES = ["lx", "lw", "xin", "pin", "snd", "p1", "p3", "ac", "vh", "py", "vp", "vy", "st"] + ["wr%d" % i for i in range(9)]
+SEMAPHORES = ["lx", "lw", "xin", "pin", "hin", "snd", "p1", "p3", "ac", "vh", "py", "vp", "vy", "st"] + ["wr%d" % i for i in range(9)]
 
 
 def _plan(T, topo):
@@ -42,36 +46,83 @@ def _plan(T, topo):
     for name, grp in (("A", A), ("M", M), ("B", B), ("Z", Z)):
         for i, c in enumerate(grp):
             role[c] = (name, i)
-    send = {}
+    direct, relay = {}, {}
     for i, a in enumerate(A):
-        send[a] = [Z[(i + k) % n] for k in range(n)] + [A[(i + k) % n] for k in range(1, n)]
+        direct[a] = [Z[(i + k) % n] for k in range(n)]
+        relay[a] = [A[(i + k) % n] for k in range(1, n)]
     ring = M + B
     for i, c in enumerate(ring):
-        send[c] = [ring[(i + k) % len(ring)] for k in range(1, len(ring))]
+        order = [ring[(i + k) % len(ring)] for k in range(1, len(ring))]
+        direct[c], relay[c] = order[:NDIRECT], order[NDIRECT:]
+    helper = {}
+    for c in ranks:
+        base = topo.host(c) * topo.CORES_PER_HOST
+        helper[c] = [w for w in range(base, base + topo.CORES_PER_HOST)
+                     if topo.chip(w) == topo.chip(c) and topo.die(w) != topo.die(c) and w not in role
+                     and topo.may_write(c, w) and all(topo.may_write(w, d) for d in relay[c])][0]
+    for c in ranks:
+        role[helper[c]] = ("H", c)
     guest_to, part_to = {}, {}
     for i in range(n):
         guest_to[A[i]], guest_to[M[i]], guest_to[B[i]] = M[i], A[i], Z[i]
         part_to[A[i]], part_to[M[i]], part_to[Z[i]] = M[i], A[i], B[i]
-    return role, send, guest_to, part_to
+    return role, direct, relay, helper, guest_to, part_to
 
 
-def _arrivals(send, d):
-    return sorted((s for s in send if d in send[s]), key=lambda s: (send[s].index(d), s))
+def _arrivals(direct, relay, d):
+    t = []
+    for s in direct:
+        if d in direct[s]:
+            t.append((2.0 + direct[s].index(d), s))
+        if d in relay[s]:
+            t.append((3.5 + relay[s].index(d), s))
+    return [s for _, s in sorted(t)]
 
 
 def _engines(mask):
     return bin(mask).count("1")
 
 
+def _common(topo, src, dests):
+    m = topo.mask(src, dests[0])
+    for d in dests:
+        m &= topo.mask(src, d)
+    return m
+
+
+def _feed_mask(topo, c, h, dests):
+    m = topo.mask(c, h) & ~_common(topo, c, dests)
+    return m if m else topo.mask(c, h)
+
+
+def _send_w(g, T, topo, core, owner, dests, direct, relay):
+    m = _common(topo, core, dests)
+    ids, dsts = [], []
+    for d in dests:
+        rid, pid = topo.addr(d, core)
+        slot = _arrivals(direct, relay, d).index(owner)
+        ids.append(DstId(rid=rid, pnc=pid))
+        dsts.append(T.wl[:, slot * WW:(slot + 1) * WW])
+    g.remote_dma_fused([RemoteDMATransfer(dst_ids=ids, dma_engine_mask=m, remote_sem=T.sem["wr%d" % T.rank_of(owner)],
+                                          srcs=[T.wo[:]], dsts=dsts, alu_op=0)], local_sem=T.sem.snd)
+    return _engines(m)
+
+
 def rank_program(g, core, T, topo):
-    role, send, guest_to, part_to = _plan(T, topo)
+    role, direct, relay, helper, guest_to, part_to = _plan(T, topo)
     if core not in role:
         return
     S = T.sem
     kind = role[core][0]
+
+    if kind == "H":
+        owner = role[core][1]
+        g.wait_ge(S.hin, _engines(_feed_mask(topo, owner, core, direct[owner])))
+        g.wait_ge(S.snd, _send_w(g, T, topo, core, owner, relay[owner], direct, relay))
+        return
+
     is_rank = kind != "Z"
     hosts_guest = kind in ("A", "M")
-    n = 2 * D if hosts_guest else D
     sent = 0
 
     if is_rank:
@@ -88,69 +139,76 @@ def rank_program(g, core, T, topo):
         g.wait_ge(S.lx, 16)
         g.remote_dma(T.xb[:, col:col + D], T.xb[:, 0:D], S.xin, S.snd, pid, rid, m)
         sent += _engines(m)
-        m = topo.mask(core, send[core][0])
-        ids, dsts = [], []
-        for d in send[core]:
-            m &= topo.mask(core, d)
-            rid, pid = topo.addr(d, core)
-            slot = _arrivals(send, d).index(core)
-            ids.append(DstId(rid=rid, pnc=pid))
-            dsts.append(T.wl[:, slot * WW:(slot + 1) * WW])
+        h = helper[core]
+        rid, pid = topo.addr(h, core)
+        m = _feed_mask(topo, core, h, direct[core])
         g.wait_ge(S.lw, 48)
-        g.remote_dma_fused([RemoteDMATransfer(dst_ids=ids, dma_engine_mask=m, remote_sem=S["wr%d" % T.rank_of(core)],
-                                              srcs=[T.wo[:]], dsts=dsts, alu_op=0)], local_sem=S.snd)
+        g.remote_dma(T.wo[:], T.wo[:], S.hin, S.snd, pid, rid, m)
         sent += _engines(m)
+        sent += _send_w(g, T, topo, core, core, direct[core], direct, relay)
 
-    batches = []
-    first = []
+    experts = []
     if is_rank:
-        first += [(S.lx, 16), (S.lw, 48)]
+        experts.append(([(S.lw, 48)], T.wo, 0))
+    for slot, s in enumerate(_arrivals(direct, relay, core)):
+        m = _common(topo, s, direct[s]) if core in direct[s] else _common(topo, helper[s], relay[s])
+        experts.append(([(S["wr%d" % T.rank_of(s)], _engines(m))], T.wl, slot * WW))
+    E = len(experts)
+    landed_x = []
     if hosts_guest or not is_rank:
         src = [s for s in guest_to if guest_to[s] == core][0]
-        first.append((S.xin, _engines(topo.mask(src, core))))
-    if is_rank:
-        batches.append((first, T.wo, 0))
-        first = []
-    for slot, s in enumerate(_arrivals(send, core)):
-        m = topo.mask(s, send[s][0])
-        for d in send[s]:
-            m &= topo.mask(s, d)
-        batches.append((first + [(S["wr%d" % T.rank_of(s)], _engines(m))], T.wl, slot * WW))
-        first = []
-    K = len(batches)
-    X = T.xb[:, 0:n]
-    z1, z3 = [T.z1a, T.z1b], [T.z3a, T.z3b]
+        landed_x = [(S.xin, _engines(topo.mask(src, core)))]
 
-    def down(k):
-        o = (k % 2) * 2 * D
-        buf, c0 = batches[k][1], batches[k][2]
-        g.tensor.wait_ge(S.vh, k + 1)
-        g.tensor.matmul(T.ya[:, 0:n], buf[:, c0 + 2 * D:c0 + WW], T.hb[:, o:o + n], k == 0, k == K - 1).then_inc(S.py, 1)
+    own = lambda k: (experts[k][0] + ([(S.lx, 16)] if is_rank else landed_x), experts[k][1], experts[k][2], 0, "ya")
+    guest = lambda k: (experts[k][0] + landed_x, experts[k][1], experts[k][2], D, "yg")
+    if hosts_guest:
+        jobs, late = [own(0), guest(0)], 1
+        for k in range(1, E):
+            jobs.append(guest(k))
+            if k - LAG >= late:
+                jobs.append(own(late))
+                late += 1
+        jobs += [own(k) for k in range(late, E)]
+    else:
+        jobs = [own(k) for k in range(E)]
+    J = len(jobs)
+    part_bank = "yg" if hosts_guest else "ya"
+    of_bank = lambda bank: [j for j in range(J) if jobs[j][4] == bank]
+    part_last = of_bank(part_bank)[-1] if core in part_to else -1
+    z1, z3 = [T.z1a, T.z1b, T.z1c], [T.z3a, T.z3b, T.z3c]
 
-    for k in range(K):
-        waits, buf, c0 = batches[k]
-        o = (k % 2) * 2 * D
+    def down(j):
+        o = (j % NB) * D
+        buf, c0, bank = jobs[j][1], jobs[j][2], jobs[j][4]
+        mine = of_bank(bank)
+        g.tensor.wait_ge(S.vh, j + 1)
+        g.tensor.matmul(T[bank][:, 0:D], buf[:, c0 + 2 * D:c0 + WW], T.hb[:, o:o + D], j == mine[0], j == mine[-1]).then_inc(S.py, 1)
+        if j == part_last:
+            g.vector.wait_ge(S.py, j + 1)
+            g.vector.tensor_copy(T.po[:], T[part_bank][:, 0:D]).then_inc(S.vp, 1)
+
+    for j in range(J):
+        waits, buf, c0, xc, bank = jobs[j]
+        o = (j % NB) * D
         for sem, val in waits:
             g.tensor.wait_ge(sem, val)
-        g.tensor.matmul(z1[k % 2][:, 0:n], buf[:, c0:c0 + D], X, True, True).then_inc(S.p1, 1)
-        g.tensor.matmul(z3[k % 2][:, 0:n], buf[:, c0 + D:c0 + 2 * D], X, True, True).then_inc(S.p3, 1)
-        if k >= 1:
-            down(k - 1)
-        g.scalar.wait_ge(S.p1, k + 1)
-        if k >= 2:
-            g.scalar.wait_ge(S.vh, k - 1)
-        g.scalar.activation(T.sl[:, o:o + n], z1[k % 2][:, 0:n], ActivationFunctionType.Silu).then_inc(S.ac, 1)
-        g.vector.wait_ge(S.ac, k + 1)
-        g.vector.wait_ge(S.p3, k + 1)
-        if k >= 2:
-            g.vector.wait_ge(S.py, k - 1)
-        g.vector.tensor_tensor(T.hb[:, o:o + n], T.sl[:, o:o + n], z3[k % 2][:, 0:n], AluOpType.mult).then_inc(S.vh, 1)
-    down(K - 1)
+        g.tensor.matmul(z1[j % NB][:, 0:D], buf[:, c0:c0 + D], T.xb[:, xc:xc + D], True, True).then_inc(S.p1, 1)
+        g.tensor.matmul(z3[j % NB][:, 0:D], buf[:, c0 + D:c0 + 2 * D], T.xb[:, xc:xc + D], True, True).then_inc(S.p3, 1)
+        if j >= NB - 1:
+            down(j - (NB - 1))
+        g.scalar.wait_ge(S.p1, j + 1)
+        if j >= NB:
+            g.scalar.wait_ge(S.vh, j - NB + 1)
+        g.scalar.activation(T.sl[:, o:o + D], z1[j % NB][:, 0:D], ActivationFunctionType.Silu).then_inc(S.ac, 1)
+        g.vector.wait_ge(S.ac, j + 1)
+        g.vector.wait_ge(S.p3, j + 1)
+        if j >= NB:
+            g.vector.wait_ge(S.py, j - NB + 1)
+        g.vector.tensor_tensor(T.hb[:, o:o + D], T.sl[:, o:o + D], z3[j % NB][:, 0:D], AluOpType.mult).then_inc(S.vh, 1)
+    for j in range(max(0, J - (NB - 1)), J):
+        down(j)
 
-    g.vector.wait_ge(S.py, K)
     if core in part_to:
-        c0 = D if hosts_guest else 0
-        g.vector.tensor_copy(T.po[:], T.ya[:, c0:c0 + D]).then_inc(S.vp, 1)
         d = part_to[core]
         rid, pid = topo.addr(d, core)
         m = topo.mask(core, d)
@@ -158,6 +216,7 @@ def rank_program(g, core, T, topo):
         g.remote_dma(T.pl[:], T.po[:], S.pin, S.snd, pid, rid, m)
         sent += _engines(m)
 
+    g.vector.wait_ge(S.py, J)
     if is_rank:
         src = [s for s in part_to if part_to[s] == core][0]
         g.vector.wait_ge(S.pin, _engines(topo.mask(src, core)))

from concourse.bass import DstId, RemoteDMATransfer
from concourse.mybir import AluOpType, ActivationFunctionType

D = 128
WW = 3 * D
NSLOT = 5
NDIRECT = 3
LAG = 2
NB = 3

SCRATCH = {
    "xb": ("sbuf", [D, 2 * D], "bfloat16"),
    "wo": ("sbuf", [D, WW], "bfloat16"),
    "wl": ("sbuf", [D, NSLOT * WW], "bfloat16"),
    "sl": ("sbuf", [D, NB * D], "float32"),
    "hb": ("sbuf", [D, NB * D], "bfloat16"),
    "po": ("sbuf", [D, D], "bfloat16"),
    "pl": ("sbuf", [D, D], "bfloat16"),
    "yb": ("sbuf", [D, D], "bfloat16"),
    "z1a": ("psum", [D, 512], "float32"), "z1b": ("psum", [D, 512], "float32"), "z1c": ("psum", [D, 512], "float32"),
    "z3a": ("psum", [D, 512], "float32"), "z3b": ("psum", [D, 512], "float32"), "z3c": ("psum", [D, 512], "float32"),
    "ya": ("psum", [D, 512], "float32"),
    "yg": ("psum", [D, 512], "float32"),
}
SEMAPHORES = ["lx", "lw", "xin", "pin", "hin", "snd", "p1", "p3", "ac", "vh", "py", "vp", "vy", "st"] + ["wr%d" % i for i in range(9)]


def _plan(T, topo):
    ranks = list(T.cores)
    both = lambda a, b: topo.may_write(a, b) and topo.may_write(b, a)
    hosts = sorted(set(topo.host(c) for c in ranks))
    of = lambda h: sorted((c for c in ranks if topo.host(c) == h), key=topo.chip)
    hub = [h for h in hosts if all(both(a, b) for a in of(h) for b in ranks if a != b)][0]
    ends = [h for h in hosts if h != hub]
    hb = [h for h in ends if topo.rack(h) == topo.rack(hub)][0]
    ha = [h for h in ends if h != hb][0]
    A, M, B = of(ha), of(hub), of(hb)
    Z = []
    for b in B:
        for h in range(4):
            z = b + (h - topo.host(b)) * topo.CORES_PER_HOST
            if h not in hosts and both(b, z) and all(topo.may_write(a, z) and topo.same_plane(a, z) for a in A):
                Z.append(z)
    n = len(A)
    role = {}
    for name, grp in (("A", A), ("M", M), ("B", B), ("Z", Z)):
        for i, c in enumerate(grp):
            role[c] = (name, i)
    direct, relay = {}, {}
    for i, a in enumerate(A):
        direct[a] = [Z[(i + k) % n] for k in range(n)]
        relay[a] = [A[(i + k) % n] for k in range(1, n)]
    ring = M + B
    for i, c in enumerate(ring):
        order = [ring[(i + k) % len(ring)] for k in range(1, len(ring))]
        direct[c], relay[c] = order[:NDIRECT], order[NDIRECT:]
    helper = {}
    for c in ranks:
        base = topo.host(c) * topo.CORES_PER_HOST
        helper[c] = [w for w in range(base, base + topo.CORES_PER_HOST)
                     if topo.chip(w) == topo.chip(c) and topo.die(w) != topo.die(c) and w not in role
                     and topo.may_write(c, w) and all(topo.may_write(w, d) for d in relay[c])][0]
    for c in ranks:
        role[helper[c]] = ("H", c)
    guest_to, part_to = {}, {}
    for i in range(n):
        guest_to[A[i]], guest_to[M[i]], guest_to[B[i]] = M[i], A[i], Z[i]
        part_to[A[i]], part_to[M[i]], part_to[Z[i]] = M[i], A[i], B[i]
    return role, direct, relay, helper, guest_to, part_to


def _arrivals(direct, relay, d):
    t = []
    for s in direct:
        if d in direct[s]:
            t.append((2.0 + direct[s].index(d), s))
        if d in relay[s]:
            t.append((3.5 + relay[s].index(d), s))
    return [s for _, s in sorted(t)]


def _engines(mask):
    return bin(mask).count("1")


def _common(topo, src, dests):
    m = topo.mask(src, dests[0])
    for d in dests:
        m &= topo.mask(src, d)
    return m


def _feed_mask(topo, c, h, dests):
    m = topo.mask(c, h) & ~_common(topo, c, dests)
    return m if m else topo.mask(c, h)


def _send_w(g, T, topo, core, owner, dests, direct, relay):
    m = _common(topo, core, dests)
    ids, dsts = [], []
    for d in dests:
        rid, pid = topo.addr(d, core)
        slot = _arrivals(direct, relay, d).index(owner)
        ids.append(DstId(rid=rid, pnc=pid))
        dsts.append(T.wl[:, slot * WW:(slot + 1) * WW])
    g.remote_dma_fused([RemoteDMATransfer(dst_ids=ids, dma_engine_mask=m, remote_sem=T.sem["wr%d" % T.rank_of(owner)],
                                          srcs=[T.wo[:]], dsts=dsts, alu_op=0)], local_sem=T.sem.snd)
    return _engines(m)


def rank_program(g, core, T, topo):
    role, direct, relay, helper, guest_to, part_to = _plan(T, topo)
    if core not in role:
        return
    S = T.sem
    kind = role[core][0]

    if kind == "H":
        owner = role[core][1]
        g.wait_ge(S.hin, _engines(_feed_mask(topo, owner, core, direct[owner])))
        g.wait_ge(S.snd, _send_w(g, T, topo, core, owner, relay[owner], direct, relay))
        return

    is_rank = kind != "Z"
    hosts_guest = kind in ("A", "M")
    sent = 0

    if is_rank:
        g.sync.dma_start(T.xb[:, 0:D], T.x[:]).then_inc(S.lx, 16)
        g.scalar.dma_start(T.wo[:, 0:D], T.w1[:]).then_inc(S.lw, 16)
        g.sync.dma_start(T.wo[:, D:2 * D], T.w3[:]).then_inc(S.lw, 16)
        g.scalar.dma_start(T.wo[:, 2 * D:WW], T.w2[:]).then_inc(S.lw, 16)

    if is_rank:
        d = guest_to[core]
        rid, pid = topo.addr(d, core)
        m = topo.mask(core, d)
        col = 0 if role[d][0] == "Z" else D
        g.wait_ge(S.lx, 16)
        g.remote_dma(T.xb[:, col:col + D], T.xb[:, 0:D], S.xin, S.snd, pid, rid, m)
        sent += _engines(m)
        h = helper[core]
        rid, pid = topo.addr(h, core)
        m = _feed_mask(topo, core, h, direct[core])
        g.wait_ge(S.lw, 48)
        g.remote_dma(T.wo[:], T.wo[:], S.hin, S.snd, pid, rid, m)
        sent += _engines(m)
        sent += _send_w(g, T, topo, core, core, direct[core], direct, relay)

    experts = []
    if is_rank:
        experts.append(([(S.lw, 48)], T.wo, 0))
    for slot, s in enumerate(_arrivals(direct, relay, core)):
        m = _common(topo, s, direct[s]) if core in direct[s] else _common(topo, helper[s], relay[s])
        experts.append(([(S["wr%d" % T.rank_of(s)], _engines(m))], T.wl, slot * WW))
    E = len(experts)
    landed_x = []
    if hosts_guest or not is_rank:
        src = [s for s in guest_to if guest_to[s] == core][0]
        landed_x = [(S.xin, _engines(topo.mask(src, core)))]

    own = lambda k: (experts[k][0] + ([(S.lx, 16)] if is_rank else landed_x), experts[k][1], experts[k][2], 0, "ya")
    guest = lambda k: (experts[k][0] + landed_x, experts[k][1], experts[k][2], D, "yg")
    if hosts_guest:
        jobs, late = [own(0), guest(0)], 1
        for k in range(1, E):
            jobs.append(guest(k))
            if k - LAG >= late:
                jobs.append(own(late))
                late += 1
        jobs += [own(k) for k in range(late, E)]
    else:
        jobs = [own(k) for k in range(E)]
    J = len(jobs)
    part_bank = "yg" if hosts_guest else "ya"
    of_bank = lambda bank: [j for j in range(J) if jobs[j][4] == bank]
    part_last = of_bank(part_bank)[-1] if core in part_to else -1
    z1, z3 = [T.z1a, T.z1b, T.z1c], [T.z3a, T.z3b, T.z3c]

    def down(j):
        o = (j % NB) * D
        buf, c0, bank = jobs[j][1], jobs[j][2], jobs[j][4]
        mine = of_bank(bank)
        g.tensor.wait_ge(S.vh, j + 1)
        g.tensor.matmul(T[bank][:, 0:D], buf[:, c0 + 2 * D:c0 + WW], T.hb[:, o:o + D], j == mine[0], j == mine[-1]).then_inc(S.py, 1)
        if j == part_last:
            g.vector.wait_ge(S.py, j + 1)
            g.vector.tensor_copy(T.po[:], T[part_bank][:, 0:D]).then_inc(S.vp, 1)

    for j in range(J):
        waits, buf, c0, xc, bank = jobs[j]
        o = (j % NB) * D
        for sem, val in waits:
            g.tensor.wait_ge(sem, val)
        g.tensor.matmul(z1[j % NB][:, 0:D], buf[:, c0:c0 + D], T.xb[:, xc:xc + D], True, True).then_inc(S.p1, 1)
        g.tensor.matmul(z3[j % NB][:, 0:D], buf[:, c0 + D:c0 + 2 * D], T.xb[:, xc:xc + D], True, True).then_inc(S.p3, 1)
        if j >= NB - 1:
            down(j - (NB - 1))
        g.scalar.wait_ge(S.p1, j + 1)
        if j >= NB:
            g.scalar.wait_ge(S.vh, j - NB + 1)
        g.scalar.activation(T.sl[:, o:o + D], z1[j % NB][:, 0:D], ActivationFunctionType.Silu).then_inc(S.ac, 1)
        g.vector.wait_ge(S.ac, j + 1)
        g.vector.wait_ge(S.p3, j + 1)
        if j >= NB:
            g.vector.wait_ge(S.py, j - NB + 1)
        g.vector.tensor_tensor(T.hb[:, o:o + D], T.sl[:, o:o + D], z3[j % NB][:, 0:D], AluOpType.mult).then_inc(S.vh, 1)
    for j in range(max(0, J - (NB - 1)), J):
        down(j)

    if core in part_to:
        d = part_to[core]
        rid, pid = topo.addr(d, core)
        m = topo.mask(core, d)
        g.wait_ge(S.vp, 1)
        g.remote_dma(T.pl[:], T.po[:], S.pin, S.snd, pid, rid, m)
        sent += _engines(m)

    g.vector.wait_ge(S.py, J)
    if is_rank:
        src = [s for s in part_to if part_to[s] == core][0]
        g.vector.wait_ge(S.pin, _engines(topo.mask(src, core)))
        g.vector.tensor_tensor(T.yb[:], T.ya[:, 0:D], T.pl[:], AluOpType.add).then_inc(S.vy, 1)
        g.sync.wait_ge(S.vy, 1)
        g.sync.dma_start(T.y[:], T.yb[:]).then_inc(S.st, 16)
        g.sync.wait_ge(S.st, 16)
    g.wait_ge(S.snd, sent)
